import numpy as np
import ml_dtypes


def mxq(x, axis, fmt="e4m3"):
    dtype, down = {"e4m3": (ml_dtypes.float8_e4m3fn, 7), "e5m2": (ml_dtypes.float8_e5m2, 14)}[fmt]
    v = np.moveaxis(np.asarray(x, np.float32).astype(ml_dtypes.bfloat16).astype(np.float64), axis, -1)
    blocks = v.reshape(v.shape[:-1] + (-1, 32))
    amax = np.abs(blocks).max(-1, keepdims=True)
    byte = np.maximum(np.where(amax > 0, np.frexp(amax)[1] - 1 + 127, 0) - down, 1)
    scale = np.exp2(byte - 127.0)
    codes = (blocks / scale).astype(np.float32).astype(dtype).astype(np.float64)
    return np.moveaxis((codes * scale).reshape(v.shape), -1, axis)


WIDE = False


def mx_kscale(k):
    if not WIDE:
        return np.ones(k)
    levels = np.array([10, -10, 5, -5, 0])
    if k % 512:
        return np.exp2(np.random.permutation(np.resize(levels, k // 32))).repeat(32)
    a = np.empty((k // 512, 16))
    for p in range(k // 512):
        a[p, :8] = np.random.permutation(np.resize(levels, 8))
        for g in range(8):
            far = levels[np.abs(levels - a[p, g]) >= 10]
            a[p, g + 8] = far[np.random.randint(len(far))]
    return np.exp2(a.ravel()).repeat(32)


BF16 = ml_dtypes.bfloat16


def bf(x):
    return np.asarray(x, np.float32).astype(BF16)


def f64(x):
    return np.asarray(x).astype(np.float64)


E2M1 = np.array([0.0, 0.5, 1.0, 1.5, 2.0, 3.0, 4.0, 6.0, -0.0, -0.5, -1.0, -1.5, -2.0, -3.0, -4.0, -6.0])


def pack_weight(w, fmt):
    k, n = w.shape
    w = f64(bf(w)).reshape(k // 32, 32, n)
    amax = np.abs(w).max(1)
    if fmt == "e4m3":
        byte = np.frexp(amax)[1] - 1 + 127 - 7
    else:
        mant, ex = np.frexp(amax / 6.0)
        byte = np.where(mant > 0.5, ex, ex - 1) + 127
    byte = np.clip(np.where(amax > 0, byte, 1), 1, 254)
    scaled = (w * np.exp2(127.0 - byte)[:, None, :]).reshape(k, n).astype(np.float32)
    by_word = np.ascontiguousarray(scaled.reshape(k // 512, 128, 4, n).transpose(0, 1, 3, 2))
    if fmt == "e4m3":
        words = by_word.astype(ml_dtypes.float8_e4m3fn).view(np.uint8)
    else:
        c = by_word.astype(ml_dtypes.float4_e2m1fn).view(np.uint8) & 0xF
        words = c[..., 0::2] | (c[..., 1::2] << 4)
    return np.ascontiguousarray(words), np.ascontiguousarray(byte.astype(np.uint8).reshape(k // 512, 16, n))


def unpack_weight(words, scales, fmt):
    g, p, n, _ = words.shape
    if fmt == "e4m3":
        vals = np.ascontiguousarray(words).view(ml_dtypes.float8_e4m3fn).astype(np.float64)
    else:
        nib = np.empty((g, p, n, 4), np.uint8)
        nib[..., 0::2] = words & 0xF
        nib[..., 1::2] = words >> 4
        vals = E2M1[nib]
    vals = vals * np.repeat(np.exp2(scales.astype(np.float64) - 127.0), 8, axis=1)[..., None]
    return vals.transpose(0, 1, 3, 2).reshape(g * 512, n)
def pack4(w):
    words, scales = pack_weight(w, "e2m1")
    return words.reshape(words.shape[0], 128, -1), scales


def unpack4(words, scales):
    return unpack_weight(words.reshape(words.shape[0], 128, -1, 2), scales, "e2m1")


def planes(Y):
    n, m = Y.shape
    b = f64(bf(Y)).reshape(n // 32, 32, m)
    amax = np.abs(b).max(1)
    byte = np.clip(np.where(amax > 0, np.frexp(amax)[1] - 1 + 127 - 7, 1), 1, 254)
    codes = (b * np.exp2(127.0 - byte)[:, None, :]).reshape(n, m).astype(np.float32).astype(ml_dtypes.float8_e4m3fn).view(np.uint8)
    words = codes.reshape(n // 512, 128, 4, m).transpose(0, 1, 3, 2)
    return np.ascontiguousarray(words), np.ascontiguousarray(byte.astype(np.uint8).reshape(n // 512, 16, m))


B, I, F, N = 2048, 1536, 512, 1024

def setup_inputs():
    rn = np.random.randn
    s = mx_kscale(I)
    t = mx_kscale(F)
    size = np.exp(0.8 * rn(B))
    positions = size[:, None] * rn(B, I) / np.sqrt(I)
    sens = rn(I, F)
    pos_words, pos_scales = pack4(positions.T * s[:, None])
    sens_words, sens_scales = pack4(sens / s[:, None])
    return {
        "pos_words": pos_words,
        "pos_scales": pos_scales,
        "sens_words": sens_words,
        "sens_scales": sens_scales,
        "hedge": bf(0.3 * size[:, None] * rn(B, F)),
        "factor_scale": bf(np.exp(0.3 * rn(F)) * t),
        "shocks": bf(rn(F, N) / np.sqrt(F) / t[:, None]),
        "half_gamma": bf(0.15 * rn(B) / size),
        "cap": bf(1.5 * size * np.exp(0.1 * rn(B))),
    }

def reference(pos_words, pos_scales, sens_words, sens_scales, hedge, factor_scale, shocks, half_gamma, cap):
    P = unpack4(pos_words, pos_scales)
    S = unpack4(sens_words, sens_scales)
    E = P.T @ S
    X = (E + f64(hedge)) * f64(factor_scale)
    D = mxq(X, 1, "e4m3") @ mxq(f64(shocks), 0, "e4m3")
    L = D + f64(half_gamma)[:, None] * (D * D)
    y = np.minimum(L, f64(cap)[:, None])
    Y = y
    words, scales = planes(Y)
    return y, words, scales

@@ -1,0 +1,276 @@
+from contextlib import ExitStack
+
+import concourse.mybir as mybir
+from concourse.masks import make_identity
+
+B, I, F, N = 2048, 1536, 512, 1024
+FLOPS = 2 * B * I * F + 2 * B * F * N
+
+F32 = mybir.dt.float32
+BF16 = mybir.dt.bfloat16
+I32 = mybir.dt.int32
+U32 = mybir.dt.uint32
+U8 = mybir.dt.uint8
+FP8X4 = mybir.dt.float8_e4m3fn_x4
+FP4X4 = mybir.dt.float4_e2m1fn_x4
+ALU = mybir.AluOpType
+ACT = mybir.ActivationFunctionType
+
+P = 128
+PACK = 4
+PASSES = I // (P * PACK)
+GROUP = P * PACK
+GROUPS = B // GROUP
+HALF = 512
+HALVES = N // HALF
+TILES = GROUPS * PACK
+STEPS = GROUPS * HALVES * PACK
+UNITS = GROUPS * HALVES
+PIECE = HALF // PACK
+STAGE1_ORDER = [("add", 0), ("add", 1), ("mul", 0), ("add", 2), ("mul", 1), ("add", 3), ("mul", 2), ("mul", 3)]
+LEAD = 10
+LOWEST = -3.4028234663852886e38
+
+
+def tile_book_scenario_losses_k5_kernel(
+    tc, pos_words, pos_scales, sens_words, sens_scales, hedge, factor_scale, shocks, half_gamma, cap, out_0, out_1, out_2
+):
+    nc = tc.nc
+    with ExitStack() as ctx:
+        keep = ctx.enter_context(tc.tile_pool(name="keep", bufs=1))
+        work = ctx.enter_context(tc.tile_pool(name="work", bufs=2))
+        psum = ctx.enter_context(tc.psum_pool(name="psum", bufs=2))
+        ctx.enter_context(tc.manual_schedule())
+
+        s_plane = keep.tile([P, PASSES, F], U8, align_bytes=64)
+        p_plane0 = keep.tile([P, PASSES, GROUP], U8, align_bytes=64)
+        p_plane_rest = keep.tile([P, PASSES, B - GROUP], U8, align_bytes=64)
+        for plane in (s_plane, p_plane0, p_plane_rest):
+            nc.vector.memset(plane[:].bitcast(I32), 0)
+
+        def load_plane(queue, plane, rows):
+            for q in range(4):
+                queue.dma_start(
+                    out=plane[32 * q : 32 * q + 4, :, :].bitcast(I32),
+                    in_=rows[:, 4 * q : 4 * q + 4, :].rearrange("g r n -> r g n").bitcast(I32),
+                )
+
+        s_words = keep.tile([P, PASSES, 2 * F], U8, align_bytes=64)
+        p_words = [keep.tile([P, PASSES, 2 * GROUP], U8, align_bytes=64, name="p_words%d" % g) for g in range(GROUPS)]
+        hedge_sb = [keep.tile([P, PACK, F], BF16, name="hedge%d" % g) for g in range(GROUPS)]
+        shock_raw = [keep.tile([P, PACK, HALF], BF16, name="shock_raw%d" % h) for h in range(HALVES)]
+        fs_sb = keep.tile([P, PACK], BF16)
+        gamma_bf = keep.tile([P, GROUPS, PACK], BF16)
+        cap_bf = keep.tile([P, GROUPS, PACK], BF16)
+
+        def load_pos(g):
+            nc.sync.dma_start(
+                out=p_words[g][:].bitcast(I32),
+                in_=pos_words[:, :, 2 * GROUP * g : 2 * GROUP * (g + 1)].rearrange("g p n -> p g n").bitcast(I32),
+            )
+
+        def load_hedge(g):
+            nc.sync.dma_start(
+                out=hedge_sb[g][:], in_=hedge[GROUP * g : GROUP * (g + 1), :].rearrange("(j b) f -> b j f", b=P)
+            )
+
+        def load_shocks(h):
+            nc.sync.dma_start(
+                out=shock_raw[h][:], in_=shocks[:, HALF * h : HALF * (h + 1)].rearrange("(p t) n -> p t n", t=PACK)
+            )
+
+        load_plane(nc.scalar, s_plane, sens_scales)
+        nc.sync.dma_start(out=s_words[:].bitcast(I32), in_=sens_words.rearrange("g p n -> p g n").bitcast(I32))
+        load_pos(0)
+        load_plane(nc.scalar, p_plane0, pos_scales[:, :, 0:GROUP])
+        load_hedge(0)
+        load_shocks(0)
+        nc.sync.dma_start(out=fs_sb[:], in_=factor_scale.rearrange("(p t) -> p t", t=PACK))
+        load_pos(1)
+        load_plane(nc.sync, p_plane_rest, pos_scales[:, :, GROUP:B])
+        load_hedge(1)
+        nc.sync.dma_start(out=gamma_bf[:], in_=half_gamma.rearrange("(g p t) -> p g t", p=P, t=PACK))
+        nc.sync.dma_start(out=cap_bf[:], in_=cap.rearrange("(g p t) -> p g t", p=P, t=PACK))
+        load_shocks(1)
+        for g in range(2, GROUPS):
+            load_pos(g)
+            load_hedge(g)
+
+        ident = keep.tile([P, P], F32)
+        make_identity(nc, ident[:])
+        gamma_sb = keep.tile([P, GROUPS, PACK], F32)
+        cap_sb = keep.tile([P, GROUPS, PACK], F32)
+        nc.gpsimd.tensor_copy(out=gamma_sb[:], in_=gamma_bf[:])
+        nc.gpsimd.tensor_copy(out=cap_sb[:], in_=cap_bf[:])
+
+        shock_bf = [keep.tile([P, HALF, PACK], BF16, align_bytes=64, name="shock_bf%d" % h) for h in range(HALVES)]
+        shock_codes = [keep.tile([P, HALF], U32, align_bytes=64, name="shock_codes%d" % h) for h in range(HALVES)]
+        shock_plane = [keep.tile([P, HALF], U8, align_bytes=64, name="shock_plane%d" % h) for h in range(HALVES)]
+
+        def interleave(copy, dst, src):
+            copy(out=dst.rearrange("p (c i) t -> p c t i", i=4), in_=src.rearrange("p t (c i) -> p c t i", i=4))
+
+        for h in range(HALVES):
+            interleave(nc.scalar.copy, shock_bf[h][:], shock_raw[h][:])
+
+        def quantize(codes, plane, grouped):
+            nc.vector.quantize_mx(out=codes.bitcast(FP8X4), scales=plane, in_=grouped.rearrange("p n t -> p (n t)"))
+
+        expo, turned, x_bf, x_codes, x_plane = {}, {}, {}, {}, {}
+
+        def exposures(i):
+            g, j = divmod(i, PACK)
+            expo[i] = psum.tile([P, F], F32, name="expo", bufs=2)
+            plane = p_plane0[:, :, P * j : P * (j + 1)] if g == 0 else p_plane_rest[:, :, P * (i - PACK) : P * (i - PACK + 1)]
+            for c in range(PASSES):
+                nc.tensor.matmul_mx(
+                    out=expo[i][:],
+                    lhsT=p_words[g][:, c, 2 * P * j : 2 * P * (j + 1)].bitcast(FP4X4),
+                    lhsT_scale=plane[:, c, :],
+                    rhs=s_words[:, c, :].bitcast(FP4X4),
+                    rhs_scale=s_plane[:, c, :],
+                    start=(c == 0),
+                    stop=(c == PASSES - 1),
+                )
+
+        def add_hedge(i):
+            g, j = divmod(i, PACK)
+            summed = work.tile([P, PACK, P], F32, name="summed", bufs=2)
+            nc.vector.tensor_tensor(
+                out=summed[:].rearrange("b t (c i) -> b c t i", i=4),
+                in0=expo[i][:].rearrange("b (c i t) -> b c t i", i=4, t=PACK),
+                in1=hedge_sb[g][:, j, :].rearrange("b (c i t) -> b c t i", i=4, t=PACK),
+                op=ALU.add,
+            )
+            turned[i] = psum.tile([P, PACK, P], F32, name="turned", bufs=2)
+            for t in range(PACK):
+                nc.tensor.transpose(turned[i][:, t, :], summed[:, t, :], ident[:])
+            if i + 2 < TILES:
+                exposures(i + 2)
+
+        def scale_factors(i):
+            g, j = divmod(i, PACK)
+            if j == 0:
+                x_bf[g] = work.tile([P, GROUP, PACK], BF16, align_bytes=64, name="x_bf", bufs=2)
+            nc.vector.tensor_tensor(
+                out=x_bf[g][:].rearrange("p (u j m) t -> p j u m t", u=PACK, j=PACK)[:, j],
+                in0=turned[i][:].rearrange("p t (m u) -> p u m t", u=PACK),
+                in1=fs_sb[:].unsqueeze(1).unsqueeze(1).to_broadcast([P, PACK, P // PACK, PACK]),
+                op=ALU.mult,
+            )
+
+        def quantize_x(g):
+            x_codes[g] = work.tile([P, GROUP], U32, align_bytes=64, name="x_codes", bufs=2)
+            x_plane[g] = work.tile([P, GROUP], U8, align_bytes=64, name="x_plane", bufs=2)
+            quantize(x_codes[g][:], x_plane[g][:], x_bf[g][:])
+
+        linear, factor, y_f32, y_bf = {}, {}, {}, {}
+        y_plane = keep.tile([P, N], U8, align_bytes=64)
+
+        def where(n):
+            u, t = divmod(n, PACK)
+            g, h = divmod(u, HALVES)
+            return u, g, h, t
+
+        def y_rows(u):
+            g, h = divmod(u, HALVES)
+            return out_0[GROUP * g : GROUP * (g + 1), HALF * h : HALF * (h + 1)].rearrange("(p t) m -> p t m", t=PACK)
+
+        def linear_losses(n):
+            u, g, h, t = where(n)
+            linear[n] = psum.tile([P, HALF], F32, name="linear", bufs=4)
+            nc.tensor.matmul_mx(
+                out=linear[n][:],
+                lhsT=x_codes[g][:, P * t : P * (t + 1)].bitcast(FP8X4),
+                lhsT_scale=x_plane[g][:, P * t : P * (t + 1)],
+                rhs=shock_codes[h][:].bitcast(FP8X4),
+                rhs_scale=shock_plane[h][:],
+                start=True,
+                stop=True,
+            )
+
+        def quad_factor(n):
+            u, g, h, t = where(n)
+            factor[n] = work.tile([P, HALF], F32, name="factor", bufs=3)
+            nc.scalar.activation(
+                out=factor[n][:], in_=linear[n][:], func=ACT.Identity, scale=gamma_sb[:, g, t : t + 1], bias=1.0
+            )
+
+        def losses(n):
+            u, g, h, t = where(n)
+            if t == 0:
+                y_f32[u] = work.tile([P, PACK, HALF], F32, name="y_f32", bufs=3)
+            nc.vector.tensor_tensor(out=y_f32[u][:, t, :], in0=linear[n][:], in1=factor[n][:], op=ALU.mult)
+
+        def clip(n):
+            u, g, h, t = where(n)
+            engine = nc.vector if n == STEPS - 1 else nc.gpsimd
+            engine.tensor_scalar(
+                out=y_f32[u][:, t, :],
+                in0=y_f32[u][:, t, :],
+                scalar1=cap_sb[:, g, t : t + 1],
+                scalar2=LOWEST,
+                op0=ALU.min,
+                op1=ALU.max,
+            )
+            if u == UNITS - 1:
+                nc.sync.dma_start(out=y_rows(u)[:, t, :], in_=y_f32[u][:, t, :])
+            elif t == PACK - 1:
+                nc.sync.dma_start(out=y_rows(u), in_=y_f32[u][:])
+
+        def round_piece(copy, u, q):
+            if q == 0:
+                y_bf[u] = work.tile([P, HALF, PACK], BF16, align_bytes=64, name="y_bf", bufs=2)
+            cols = slice(PIECE * q, PIECE * (q + 1))
+            interleave(copy, y_bf[u][:, cols, :], y_f32[u][:, :, cols])
+
+        def quantize_y(u):
+            g, h = divmod(u, HALVES)
+            y_codes = work.tile([P, HALF], U32, align_bytes=64, name="y_codes", bufs=2)
+            quantize(y_codes[:], y_plane[4 * g : P, HALF * h : HALF * (h + 1)], y_bf[u][:])
+            nc.sync.dma_start(
+                out=out_1[g].rearrange("p m t -> p (m t)")[:, 4 * HALF * h : 4 * HALF * (h + 1)].bitcast(I32),
+                in_=y_codes[:].bitcast(I32),
+            )
+
+        exposures(0)
+        exposures(1)
+        for n in range(-LEAD, STEPS + 1):
+            if 0 <= n + 1 < STEPS:
+                quad_factor(n + 1)
+            if 0 <= n < STEPS:
+                losses(n)
+                if n < STEPS - 1:
+                    clip(n)
+            if n == -2:
+                quantize(shock_codes[0][:], shock_plane[0][:], shock_bf[0][:])
+            if n == 1:
+                quantize(shock_codes[1][:], shock_plane[1][:], shock_bf[1][:])
+            if (n + 2) % 8 == 0 and 0 <= n + 2 < STEPS:
+                quantize_x((n + 2) // 8)
+            if n >= 10 and (n - 10) % PACK == 0:
+                quantize_y((n - 10) // PACK)
+            if n >= 5:
+                u, q = divmod(n - 5, PACK)
+                on_vector = n + LEAD >= STEPS and q % 2 == 1
+                round_piece(nc.vector.tensor_copy if on_vector else nc.scalar.copy, u, q)
+            if n == STEPS - 1:
+                clip(n)
+            if 0 <= n + 2 < STEPS:
+                linear_losses(n + 2)
+            if n + LEAD < STEPS:
+                g, k = divmod(n + LEAD, 8)
+                kind, j = STAGE1_ORDER[k]
+                (add_hedge if kind == "add" else scale_factors)(PACK * g + j)
+
+        last = UNITS - 1
+        round_piece(nc.vector.tensor_copy, last, 0)
+        round_piece(nc.scalar.copy, last, 3)
+        quantize_y(last - 1)
+        round_piece(nc.vector.tensor_copy, last, 1)
+        round_piece(nc.vector.tensor_copy, last, 2)
+        quantize_y(last)
+        for q in range(4):
+            (nc.scalar if q % 2 else nc.sync).dma_start(
+                out=out_2[:, 4 * q : 4 * q + 4, :].bitcast(I32), in_=y_plane[32 * q : 32 * q + 16, :].bitcast(I32)
+            )

@@ -27,8 +27,8 @@ TILES = GROUPS * PACK
 STEPS = GROUPS * HALVES * PACK
 UNITS = GROUPS * HALVES
 PIECE = HALF // PACK
-STAGE1_ORDER = [("add", 0), ("add", 1), ("mul", 0), ("add", 2), ("mul", 1), ("add", 3), ("mul", 2), ("mul", 3)]
-LEAD = 10
+LEAD = 13
+WARMUP = 3
 LOWEST = -3.4028234663852886e38
 
 
@@ -45,11 +45,12 @@ def tile_book_scenario_losses_k5_kernel(
         s_plane = keep.tile([P, PASSES, F], U8, align_bytes=64)
         p_plane0 = keep.tile([P, PASSES, GROUP], U8, align_bytes=64)
         p_plane_rest = keep.tile([P, PASSES, B - GROUP], U8, align_bytes=64)
-        for plane in (s_plane, p_plane0, p_plane_rest):
+        nc.gpsimd.memset(s_plane[:].bitcast(I32), 0)
+        for plane in (p_plane0, p_plane_rest):
             nc.vector.memset(plane[:].bitcast(I32), 0)
 
-        def load_plane(queue, plane, rows):
-            for q in range(4):
+        def load_plane(plane, rows, quadrants, queue=nc.sync):
+            for q in quadrants:
                 queue.dma_start(
                     out=plane[32 * q : 32 * q + 4, :, :].bitcast(I32),
                     in_=rows[:, 4 * q : 4 * q + 4, :].rearrange("g r n -> r g n").bitcast(I32),
@@ -79,19 +80,19 @@ def tile_book_scenario_losses_k5_kernel(
                 out=shock_raw[h][:], in_=shocks[:, HALF * h : HALF * (h + 1)].rearrange("(p t) n -> p t n", t=PACK)
             )
 
-        load_plane(nc.scalar, s_plane, sens_scales)
+        load_plane(s_plane, sens_scales, range(4))
         nc.sync.dma_start(out=s_words[:].bitcast(I32), in_=sens_words.rearrange("g p n -> p g n").bitcast(I32))
         load_pos(0)
-        load_plane(nc.scalar, p_plane0, pos_scales[:, :, 0:GROUP])
         load_hedge(0)
-        load_shocks(0)
         nc.sync.dma_start(out=fs_sb[:], in_=factor_scale.rearrange("(p t) -> p t", t=PACK))
+        load_plane(p_plane0, pos_scales[:, :, 0:GROUP], range(4))
         load_pos(1)
-        load_plane(nc.sync, p_plane_rest, pos_scales[:, :, GROUP:B])
+        load_shocks(0)
+        load_shocks(1)
+        load_plane(p_plane_rest, pos_scales[:, :, GROUP:B], range(4))
         load_hedge(1)
         nc.sync.dma_start(out=gamma_bf[:], in_=half_gamma.rearrange("(g p t) -> p g t", p=P, t=PACK))
         nc.sync.dma_start(out=cap_bf[:], in_=cap.rearrange("(g p t) -> p g t", p=P, t=PACK))
-        load_shocks(1)
         for g in range(2, GROUPS):
             load_pos(g)
             load_hedge(g)
@@ -100,6 +101,26 @@ def tile_book_scenario_losses_k5_kernel(
         make_identity(nc, ident[:])
         gamma_sb = keep.tile([P, GROUPS, PACK], F32)
         cap_sb = keep.tile([P, GROUPS, PACK], F32)
+        hedge_f32 = {}
+
+        def widen_hedge(i):
+            g, j = divmod(i, PACK)
+            hedge_f32[i] = work.tile([P, PACK, P], F32, name="hedge_f32", bufs=4)
+            nc.gpsimd.tensor_scalar(
+                out=hedge_f32[i][:].rearrange("b t (c i) -> b c t i", i=4),
+                in0=hedge_sb[g][:, j, :].rearrange("b (c i t) -> b c t i", i=4, t=PACK),
+                scalar1=1.0,
+                scalar2=0.0,
+                op0=ALU.mult,
+                op1=ALU.add,
+            )
+
+        def by_scalar(i):
+            return i % 4 == 3 and i >= PACK
+
+        for i in range(2 * PACK):
+            if by_scalar(i):
+                widen_hedge(i)
         nc.gpsimd.tensor_copy(out=gamma_sb[:], in_=gamma_bf[:])
         nc.gpsimd.tensor_copy(out=cap_sb[:], in_=cap_bf[:])
 
@@ -110,17 +131,22 @@ def tile_book_scenario_losses_k5_kernel(
         def interleave(copy, dst, src):
             copy(out=dst.rearrange("p (c i) t -> p c t i", i=4), in_=src.rearrange("p t (c i) -> p c t i", i=4))
 
-        for h in range(HALVES):
-            interleave(nc.scalar.copy, shock_bf[h][:], shock_raw[h][:])
+        def shock_piece(s):
+            h, q = divmod(s, 2)
+            cols = slice(256 * q, 256 * (q + 1))
+            interleave(nc.scalar.copy, shock_bf[h][:, cols, :], shock_raw[h][:, :, cols])
 
         def quantize(codes, plane, grouped):
             nc.vector.quantize_mx(out=codes.bitcast(FP8X4), scales=plane, in_=grouped.rearrange("p n t -> p (n t)"))
 
-        expo, turned, x_bf, x_codes, x_plane = {}, {}, {}, {}, {}
+        expo, addends, turned, x_bf, x_codes, x_plane = {}, {}, {}, {}, {}, {}
 
         def exposures(i):
             g, j = divmod(i, PACK)
-            expo[i] = psum.tile([P, F], F32, name="expo", bufs=2)
+            if i < PACK:
+                expo[i] = psum.tile([P, F], F32, name="linear", bufs=4)
+            else:
+                expo[i] = psum.tile([P, F], F32, name="expo", bufs=2)
             plane = p_plane0[:, :, P * j : P * (j + 1)] if g == 0 else p_plane_rest[:, :, P * (i - PACK) : P * (i - PACK + 1)]
             for c in range(PASSES):
                 nc.tensor.matmul_mx(
@@ -135,18 +161,34 @@ def tile_book_scenario_losses_k5_kernel(
 
         def add_hedge(i):
             g, j = divmod(i, PACK)
-            summed = work.tile([P, PACK, P], F32, name="summed", bufs=2)
-            nc.vector.tensor_tensor(
-                out=summed[:].rearrange("b t (c i) -> b c t i", i=4),
-                in0=expo[i][:].rearrange("b (c i t) -> b c t i", i=4, t=PACK),
-                in1=hedge_sb[g][:, j, :].rearrange("b (c i t) -> b c t i", i=4, t=PACK),
-                op=ALU.add,
-            )
+            summed = work.tile([P, PACK, P], F32, name="summed", bufs=4)
+            dst = summed[:].rearrange("b t (c i) -> b c t i", i=4)
+            src = expo[i][:].rearrange("b (c i t) -> b c t i", i=4, t=PACK)
+            if not by_scalar(i):
+                nc.vector.tensor_tensor(
+                    out=dst,
+                    in0=src,
+                    in1=hedge_sb[g][:, j, :].rearrange("b (c i t) -> b c t i", i=4, t=PACK),
+                    op=ALU.add,
+                )
+                addends[i] = [summed]
+            else:
+                nc.scalar.copy(out=dst, in_=src)
+                addends[i] = [hedge_f32[i], summed]
+
+        def turn(i):
+            parts = addends[i]
             turned[i] = psum.tile([P, PACK, P], F32, name="turned", bufs=2)
             for t in range(PACK):
-                nc.tensor.transpose(turned[i][:, t, :], summed[:, t, :], ident[:])
-            if i + 2 < TILES:
-                exposures(i + 2)
+                for part in parts:
+                    nc.tensor.matmul(
+                        turned[i][:, t, :],
+                        lhsT=part[:, t, :],
+                        rhs=ident[:],
+                        is_transpose=True,
+                        start=(part is parts[0]),
+                        stop=(part is parts[-1]),
+                    )
 
         def scale_factors(i):
             g, j = divmod(i, PACK)
@@ -162,7 +204,10 @@ def tile_book_scenario_losses_k5_kernel(
         def quantize_x(g):
             x_codes[g] = work.tile([P, GROUP], U32, align_bytes=64, name="x_codes", bufs=2)
             x_plane[g] = work.tile([P, GROUP], U8, align_bytes=64, name="x_plane", bufs=2)
-            quantize(x_codes[g][:], x_plane[g][:], x_bf[g][:])
+            width = P if g == 0 else GROUP
+            for c0 in range(0, GROUP, width):
+                cols = slice(c0, c0 + width)
+                quantize(x_codes[g][:, cols], x_plane[g][:, cols], x_bf[g][:, cols, :])
 
         linear, factor, y_f32, y_bf = {}, {}, {}, {}
         y_plane = keep.tile([P, N], U8, align_bytes=64)
@@ -191,7 +236,7 @@ def tile_book_scenario_losses_k5_kernel(
 
         def quad_factor(n):
             u, g, h, t = where(n)
-            factor[n] = work.tile([P, HALF], F32, name="factor", bufs=3)
+            factor[n] = work.tile([P, HALF], F32, name="factor", bufs=4)
             nc.scalar.activation(
                 out=factor[n][:], in_=linear[n][:], func=ACT.Identity, scale=gamma_sb[:, g, t : t + 1], bias=1.0
             )
@@ -199,7 +244,7 @@ def tile_book_scenario_losses_k5_kernel(
         def losses(n):
             u, g, h, t = where(n)
             if t == 0:
-                y_f32[u] = work.tile([P, PACK, HALF], F32, name="y_f32", bufs=3)
+                y_f32[u] = work.tile([P, PACK, HALF], F32, name="y_f32", bufs=4)
             nc.vector.tensor_tensor(out=y_f32[u][:, t, :], in0=linear[n][:], in1=factor[n][:], op=ALU.mult)
 
         def clip(n):
@@ -215,8 +260,8 @@ def tile_book_scenario_losses_k5_kernel(
             )
             if u == UNITS - 1:
                 nc.sync.dma_start(out=y_rows(u)[:, t, :], in_=y_f32[u][:, t, :])
-            elif t == PACK - 1:
-                nc.sync.dma_start(out=y_rows(u), in_=y_f32[u][:])
+            elif t % 2 == 1:
+                nc.sync.dma_start(out=y_rows(u)[:, t - 1 : t + 1, :], in_=y_f32[u][:, t - 1 : t + 1, :])
 
         def round_piece(copy, u, q):
             if q == 0:
@@ -226,49 +271,91 @@ def tile_book_scenario_losses_k5_kernel(
 
         def quantize_y(u):
             g, h = divmod(u, HALVES)
-            y_codes = work.tile([P, HALF], U32, align_bytes=64, name="y_codes", bufs=2)
+            y_codes = work.tile([P, HALF], U32, align_bytes=64, name="y_codes", bufs=4)
             quantize(y_codes[:], y_plane[4 * g : P, HALF * h : HALF * (h + 1)], y_bf[u][:])
             nc.sync.dma_start(
                 out=out_1[g].rearrange("p m t -> p (m t)")[:, 4 * HALF * h : 4 * HALF * (h + 1)].bitcast(I32),
                 in_=y_codes[:].bitcast(I32),
             )
 
-        exposures(0)
-        exposures(1)
-        for n in range(-LEAD, STEPS + 1):
-            if 0 <= n + 1 < STEPS:
-                quad_factor(n + 1)
+        warm = psum.tile([P, F], F32, name="expo", bufs=2)
+        for w in range(WARMUP):
+            nc.tensor.matmul_mx(
+                out=warm[:],
+                lhsT=s_words[:, 0, 0 : 2 * P].bitcast(FP4X4),
+                lhsT_scale=s_plane[:, 0, 0:P],
+                rhs=s_words[:, 0, :].bitcast(FP4X4),
+                rhs_scale=s_plane[:, 0, :],
+                start=True,
+                stop=True,
+            )
+
+        for i in range(PACK):
+            exposures(i)
+        for i in range(PACK):
+            add_hedge(i)
+            shock_piece(i)
+        turn(0)
+        turn(1)
+        scale_factors(0)
+        turn(2)
+        scale_factors(1)
+        turn(3)
+        exposures(4)
+        scale_factors(2)
+        scale_factors(3)
+        quantize(shock_codes[0][:], shock_plane[0][:], shock_bf[0][:])
+        quantize_x(0)
+        linear_losses(0)
+        linear_losses(1)
+        exposures(5)
+        quad_factor(0)
+        k_next = 2 * PACK
+        for n in range(-1, STEPS):
+            ks = range(k_next, min(k_next + 2, n + LEAD + 1))
+            k_next = ks.stop
+            for k in ks:
+                if k % 2 == 0 and k // 2 < TILES and by_scalar(k // 2):
+                    add_hedge(k // 2)
+            if 0 <= n + 2 < STEPS:
+                quad_factor(n + 2)
             if 0 <= n < STEPS:
                 losses(n)
                 if n < STEPS - 1:
                     clip(n)
-            if n == -2:
-                quantize(shock_codes[0][:], shock_plane[0][:], shock_bf[0][:])
-            if n == 1:
+            if n == 0:
                 quantize(shock_codes[1][:], shock_plane[1][:], shock_bf[1][:])
-            if (n + 2) % 8 == 0 and 0 <= n + 2 < STEPS:
-                quantize_x((n + 2) // 8)
-            if n >= 10 and (n - 10) % PACK == 0:
-                quantize_y((n - 10) // PACK)
-            if n >= 5:
-                u, q = divmod(n - 5, PACK)
-                on_vector = n + LEAD >= STEPS and q % 2 == 1
+            if (n + 3) % 8 == 0 and n + 3 < STEPS:
+                quantize_x((n + 3) // 8)
+            if n >= 9 and (n - 9) % PACK == 0:
+                quantize_y((n - 9) // PACK)
+            if 4 <= n:
+                u, q = divmod(n - 4, PACK)
+                on_vector = n >= 21 and q % 2 == 1 and n < STEPS - 2
                 round_piece(nc.vector.tensor_copy if on_vector else nc.scalar.copy, u, q)
             if n == STEPS - 1:
                 clip(n)
-            if 0 <= n + 2 < STEPS:
-                linear_losses(n + 2)
-            if n + LEAD < STEPS:
-                g, k = divmod(n + LEAD, 8)
-                kind, j = STAGE1_ORDER[k]
-                (add_hedge if kind == "add" else scale_factors)(PACK * g + j)
+            if 0 <= n + 3 < STEPS:
+                linear_losses(n + 3)
+            for k in ks:
+                i = k // 2
+                if k % 2 == 0 and i < TILES and not by_scalar(i):
+                    add_hedge(i)
+                if k % 2 == 1 and i < TILES:
+                    turn(i)
+                    if i + 2 < TILES:
+                        exposures(i + 2)
+                if k % 2 == 1 and PACK <= i - 1 < TILES:
+                    scale_factors(i - 1)
+                if k % 2 == 0 and 2 * PACK <= i + 2 < TILES and by_scalar(i + 2):
+                    widen_hedge(i + 2)
 
         last = UNITS - 1
-        round_piece(nc.vector.tensor_copy, last, 0)
-        round_piece(nc.scalar.copy, last, 3)
         quantize_y(last - 1)
-        round_piece(nc.vector.tensor_copy, last, 1)
+        round_piece(nc.scalar.copy, last, 0)
+        round_piece(nc.vector.tensor_copy, last, 3)
         round_piece(nc.vector.tensor_copy, last, 2)
+        round_piece(nc.scalar.copy, last, 1)
         quantize_y(last)
         for q in range(4):
             (nc.scalar if q % 2 else nc.sync).dma_start(

from contextlib import ExitStack

import concourse.mybir as mybir
from concourse.masks import make_identity

B, I, F, N = 2048, 1536, 512, 1024
FLOPS = 2 * B * I * F + 2 * B * F * N

F32 = mybir.dt.float32
BF16 = mybir.dt.bfloat16
I32 = mybir.dt.int32
U32 = mybir.dt.uint32
U8 = mybir.dt.uint8
FP8X4 = mybir.dt.float8_e4m3fn_x4
FP4X4 = mybir.dt.float4_e2m1fn_x4
ALU = mybir.AluOpType
ACT = mybir.ActivationFunctionType

P = 128
PACK = 4
PASSES = I // (P * PACK)
GROUP = P * PACK
GROUPS = B // GROUP
HALF = 512
HALVES = N // HALF
TILES = GROUPS * PACK
STEPS = GROUPS * HALVES * PACK
UNITS = GROUPS * HALVES
PIECE = HALF // PACK
LEAD = 13
WARMUP = 3
LOWEST = -3.4028234663852886e38


def tile_book_scenario_losses_k5_kernel(
    tc, pos_words, pos_scales, sens_words, sens_scales, hedge, factor_scale, shocks, half_gamma, cap, out_0, out_1, out_2
):
    nc = tc.nc
    with ExitStack() as ctx:
        keep = ctx.enter_context(tc.tile_pool(name="keep", bufs=1))
        work = ctx.enter_context(tc.tile_pool(name="work", bufs=2))
        psum = ctx.enter_context(tc.psum_pool(name="psum", bufs=2))
        ctx.enter_context(tc.manual_schedule())

        s_plane = keep.tile([P, PASSES, F], U8, align_bytes=64)
        p_plane0 = keep.tile([P, PASSES, GROUP], U8, align_bytes=64)
        p_plane_rest = keep.tile([P, PASSES, B - GROUP], U8, align_bytes=64)
        nc.gpsimd.memset(s_plane[:].bitcast(I32), 0)
        for plane in (p_plane0, p_plane_rest):
            nc.vector.memset(plane[:].bitcast(I32), 0)

        def load_plane(plane, rows, quadrants, queue=nc.sync):
            for q in quadrants:
                queue.dma_start(
                    out=plane[32 * q : 32 * q + 4, :, :].bitcast(I32),
                    in_=rows[:, 4 * q : 4 * q + 4, :].rearrange("g r n -> r g n").bitcast(I32),
                )

        s_words = keep.tile([P, PASSES, 2 * F], U8, align_bytes=64)
        p_words = [keep.tile([P, PASSES, 2 * GROUP], U8, align_bytes=64, name="p_words%d" % g) for g in range(GROUPS)]
        hedge_sb = [keep.tile([P, PACK, F], BF16, name="hedge%d" % g) for g in range(GROUPS)]
        shock_raw = [keep.tile([P, PACK, HALF], BF16, name="shock_raw%d" % h) for h in range(HALVES)]
        fs_sb = keep.tile([P, PACK], BF16)
        gamma_bf = keep.tile([P, GROUPS, PACK], BF16)
        cap_bf = keep.tile([P, GROUPS, PACK], BF16)

        def load_pos(g):
            nc.sync.dma_start(
                out=p_words[g][:].bitcast(I32),
                in_=pos_words[:, :, 2 * GROUP * g : 2 * GROUP * (g + 1)].rearrange("g p n -> p g n").bitcast(I32),
            )

        def load_hedge(g):
            nc.sync.dma_start(
                out=hedge_sb[g][:], in_=hedge[GROUP * g : GROUP * (g + 1), :].rearrange("(j b) f -> b j f", b=P)
            )

        def load_shocks(h):
            nc.sync.dma_start(
                out=shock_raw[h][:], in_=shocks[:, HALF * h : HALF * (h + 1)].rearrange("(p t) n -> p t n", t=PACK)
            )

        load_plane(s_plane, sens_scales, range(4))
        nc.sync.dma_start(out=s_words[:].bitcast(I32), in_=sens_words.rearrange("g p n -> p g n").bitcast(I32))
        load_pos(0)
        load_hedge(0)
        nc.sync.dma_start(out=fs_sb[:], in_=factor_scale.rearrange("(p t) -> p t", t=PACK))
        load_plane(p_plane0, pos_scales[:, :, 0:GROUP], range(4))
        load_pos(1)
        load_shocks(0)
        load_shocks(1)
        load_plane(p_plane_rest, pos_scales[:, :, GROUP:B], range(4))
        load_hedge(1)
        nc.sync.dma_start(out=gamma_bf[:], in_=half_gamma.rearrange("(g p t) -> p g t", p=P, t=PACK))
        nc.sync.dma_start(out=cap_bf[:], in_=cap.rearrange("(g p t) -> p g t", p=P, t=PACK))
        for g in range(2, GROUPS):
            load_pos(g)
            load_hedge(g)

        ident = keep.tile([P, P], F32)
        make_identity(nc, ident[:])
        gamma_sb = keep.tile([P, GROUPS, PACK], F32)
        cap_sb = keep.tile([P, GROUPS, PACK], F32)
        hedge_f32 = {}

        def widen_hedge(i):
            g, j = divmod(i, PACK)
            hedge_f32[i] = work.tile([P, PACK, P], F32, name="hedge_f32", bufs=4)
            nc.gpsimd.tensor_scalar(
                out=hedge_f32[i][:].rearrange("b t (c i) -> b c t i", i=4),
                in0=hedge_sb[g][:, j, :].rearrange("b (c i t) -> b c t i", i=4, t=PACK),
                scalar1=1.0,
                scalar2=0.0,
                op0=ALU.mult,
                op1=ALU.add,
            )

        def by_scalar(i):
            return i % 4 == 3 and i >= PACK

        for i in range(2 * PACK):
            if by_scalar(i):
                widen_hedge(i)
        nc.gpsimd.tensor_copy(out=gamma_sb[:], in_=gamma_bf[:])
        nc.gpsimd.tensor_copy(out=cap_sb[:], in_=cap_bf[:])

        shock_bf = [keep.tile([P, HALF, PACK], BF16, align_bytes=64, name="shock_bf%d" % h) for h in range(HALVES)]
        shock_codes = [keep.tile([P, HALF], U32, align_bytes=64, name="shock_codes%d" % h) for h in range(HALVES)]
        shock_plane = [keep.tile([P, HALF], U8, align_bytes=64, name="shock_plane%d" % h) for h in range(HALVES)]

        def interleave(copy, dst, src):
            copy(out=dst.rearrange("p (c i) t -> p c t i", i=4), in_=src.rearrange("p t (c i) -> p c t i", i=4))

        def shock_piece(s):
            h, q = divmod(s, 2)
            cols = slice(256 * q, 256 * (q + 1))
            interleave(nc.scalar.copy, shock_bf[h][:, cols, :], shock_raw[h][:, :, cols])

        def quantize(codes, plane, grouped):
            nc.vector.quantize_mx(out=codes.bitcast(FP8X4), scales=plane, in_=grouped.rearrange("p n t -> p (n t)"))

        expo, addends, turned, x_bf, x_codes, x_plane = {}, {}, {}, {}, {}, {}

        def exposures(i):
            g, j = divmod(i, PACK)
            if i < PACK:
                expo[i] = psum.tile([P, F], F32, name="linear", bufs=4)
            else:
                expo[i] = psum.tile([P, F], F32, name="expo", bufs=2)
            plane = p_plane0[:, :, P * j : P * (j + 1)] if g == 0 else p_plane_rest[:, :, P * (i - PACK) : P * (i - PACK + 1)]
            for c in range(PASSES):
                nc.tensor.matmul_mx(
                    out=expo[i][:],
                    lhsT=p_words[g][:, c, 2 * P * j : 2 * P * (j + 1)].bitcast(FP4X4),
                    lhsT_scale=plane[:, c, :],
                    rhs=s_words[:, c, :].bitcast(FP4X4),
                    rhs_scale=s_plane[:, c, :],
                    start=(c == 0),
                    stop=(c == PASSES - 1),
                )

        def add_hedge(i):
            g, j = divmod(i, PACK)
            summed = work.tile([P, PACK, P], F32, name="summed", bufs=4)
            dst = summed[:].rearrange("b t (c i) -> b c t i", i=4)
            src = expo[i][:].rearrange("b (c i t) -> b c t i", i=4, t=PACK)
            if not by_scalar(i):
                nc.vector.tensor_tensor(
                    out=dst,
                    in0=src,
                    in1=hedge_sb[g][:, j, :].rearrange("b (c i t) -> b c t i", i=4, t=PACK),
                    op=ALU.add,
                )
                addends[i] = [summed]
            else:
                nc.scalar.copy(out=dst, in_=src)
                addends[i] = [hedge_f32[i], summed]

        def turn(i):
            parts = addends[i]
            turned[i] = psum.tile([P, PACK, P], F32, name="turned", bufs=2)
            for t in range(PACK):
                for part in parts:
                    nc.tensor.matmul(
                        turned[i][:, t, :],
                        lhsT=part[:, t, :],
                        rhs=ident[:],
                        is_transpose=True,
                        start=(part is parts[0]),
                        stop=(part is parts[-1]),
                    )

        def scale_factors(i):
            g, j = divmod(i, PACK)
            if j == 0:
                x_bf[g] = work.tile([P, GROUP, PACK], BF16, align_bytes=64, name="x_bf", bufs=2)
            nc.vector.tensor_tensor(
                out=x_bf[g][:].rearrange("p (u j m) t -> p j u m t", u=PACK, j=PACK)[:, j],
                in0=turned[i][:].rearrange("p t (m u) -> p u m t", u=PACK),
                in1=fs_sb[:].unsqueeze(1).unsqueeze(1).to_broadcast([P, PACK, P // PACK, PACK]),
                op=ALU.mult,
            )

        def quantize_x(g):
            x_codes[g] = work.tile([P, GROUP], U32, align_bytes=64, name="x_codes", bufs=2)
            x_plane[g] = work.tile([P, GROUP], U8, align_bytes=64, name="x_plane", bufs=2)
            width = P if g == 0 else GROUP
            for c0 in range(0, GROUP, width):
                cols = slice(c0, c0 + width)
                quantize(x_codes[g][:, cols], x_plane[g][:, cols], x_bf[g][:, cols, :])

        linear, factor, y_f32, y_bf = {}, {}, {}, {}
        y_plane = keep.tile([P, N], U8, align_bytes=64)

        def where(n):
            u, t = divmod(n, PACK)
            g, h = divmod(u, HALVES)
            return u, g, h, t

        def y_rows(u):
            g, h = divmod(u, HALVES)
            return out_0[GROUP * g : GROUP * (g + 1), HALF * h : HALF * (h + 1)].rearrange("(p t) m -> p t m", t=PACK)

        def linear_losses(n):
            u, g, h, t = where(n)
            linear[n] = psum.tile([P, HALF], F32, name="linear", bufs=4)
            nc.tensor.matmul_mx(
                out=linear[n][:],
                lhsT=x_codes[g][:, P * t : P * (t + 1)].bitcast(FP8X4),
                lhsT_scale=x_plane[g][:, P * t : P * (t + 1)],
                rhs=shock_codes[h][:].bitcast(FP8X4),
                rhs_scale=shock_plane[h][:],
                start=True,
                stop=True,
            )

        def quad_factor(n):
            u, g, h, t = where(n)
            factor[n] = work.tile([P, HALF], F32, name="factor", bufs=4)
            nc.scalar.activation(
                out=factor[n][:], in_=linear[n][:], func=ACT.Identity, scale=gamma_sb[:, g, t : t + 1], bias=1.0
            )

        def losses(n):
            u, g, h, t = where(n)
            if t == 0:
                y_f32[u] = work.tile([P, PACK, HALF], F32, name="y_f32", bufs=4)
            nc.vector.tensor_tensor(out=y_f32[u][:, t, :], in0=linear[n][:], in1=factor[n][:], op=ALU.mult)

        def clip(n):
            u, g, h, t = where(n)
            engine = nc.vector if n == STEPS - 1 else nc.gpsimd
            engine.tensor_scalar(
                out=y_f32[u][:, t, :],
                in0=y_f32[u][:, t, :],
                scalar1=cap_sb[:, g, t : t + 1],
                scalar2=LOWEST,
                op0=ALU.min,
                op1=ALU.max,
            )
            if u == UNITS - 1:
                nc.sync.dma_start(out=y_rows(u)[:, t, :], in_=y_f32[u][:, t, :])
            elif t % 2 == 1:
                nc.sync.dma_start(out=y_rows(u)[:, t - 1 : t + 1, :], in_=y_f32[u][:, t - 1 : t + 1, :])

        def round_piece(copy, u, q):
            if q == 0:
                y_bf[u] = work.tile([P, HALF, PACK], BF16, align_bytes=64, name="y_bf", bufs=2)
            cols = slice(PIECE * q, PIECE * (q + 1))
            interleave(copy, y_bf[u][:, cols, :], y_f32[u][:, :, cols])

        def quantize_y(u):
            g, h = divmod(u, HALVES)
            y_codes = work.tile([P, HALF], U32, align_bytes=64, name="y_codes", bufs=4)
            quantize(y_codes[:], y_plane[4 * g : P, HALF * h : HALF * (h + 1)], y_bf[u][:])
            nc.sync.dma_start(
                out=out_1[g].rearrange("p m t -> p (m t)")[:, 4 * HALF * h : 4 * HALF * (h + 1)].bitcast(I32),
                in_=y_codes[:].bitcast(I32),
            )

        warm = psum.tile([P, F], F32, name="expo", bufs=2)
        for w in range(WARMUP):
            nc.tensor.matmul_mx(
                out=warm[:],
                lhsT=s_words[:, 0, 0 : 2 * P].bitcast(FP4X4),
                lhsT_scale=s_plane[:, 0, 0:P],
                rhs=s_words[:, 0, :].bitcast(FP4X4),
                rhs_scale=s_plane[:, 0, :],
                start=True,
                stop=True,
            )

        for i in range(PACK):
            exposures(i)
        for i in range(PACK):
            add_hedge(i)
            shock_piece(i)
        turn(0)
        turn(1)
        scale_factors(0)
        turn(2)
        scale_factors(1)
        turn(3)
        exposures(4)
        scale_factors(2)
        scale_factors(3)
        quantize(shock_codes[0][:], shock_plane[0][:], shock_bf[0][:])
        quantize_x(0)
        linear_losses(0)
        linear_losses(1)
        exposures(5)
        quad_factor(0)
        k_next = 2 * PACK
        for n in range(-1, STEPS):
            ks = range(k_next, min(k_next + 2, n + LEAD + 1))
            k_next = ks.stop
            for k in ks:
                if k % 2 == 0 and k // 2 < TILES and by_scalar(k // 2):
                    add_hedge(k // 2)
            if 0 <= n + 2 < STEPS:
                quad_factor(n + 2)
            if 0 <= n < STEPS:
                losses(n)
                if n < STEPS - 1:
                    clip(n)
            if n == 0:
                quantize(shock_codes[1][:], shock_plane[1][:], shock_bf[1][:])
            if (n + 3) % 8 == 0 and n + 3 < STEPS:
                quantize_x((n + 3) // 8)
            if n >= 9 and (n - 9) % PACK == 0:
                quantize_y((n - 9) // PACK)
            if 4 <= n:
                u, q = divmod(n - 4, PACK)
                on_vector = n >= 21 and q % 2 == 1 and n < STEPS - 2
                round_piece(nc.vector.tensor_copy if on_vector else nc.scalar.copy, u, q)
            if n == STEPS - 1:
                clip(n)
            if 0 <= n + 3 < STEPS:
                linear_losses(n + 3)
            for k in ks:
                i = k // 2
                if k % 2 == 0 and i < TILES and not by_scalar(i):
                    add_hedge(i)
                if k % 2 == 1 and i < TILES:
                    turn(i)
                    if i + 2 < TILES:
                        exposures(i + 2)
                if k % 2 == 1 and PACK <= i - 1 < TILES:
                    scale_factors(i - 1)
                if k % 2 == 0 and 2 * PACK <= i + 2 < TILES and by_scalar(i + 2):
                    widen_hedge(i + 2)

        last = UNITS - 1
        quantize_y(last - 1)
        round_piece(nc.scalar.copy, last, 0)
        round_piece(nc.vector.tensor_copy, last, 3)
        round_piece(nc.vector.tensor_copy, last, 2)
        round_piece(nc.scalar.copy, last, 1)
        quantize_y(last)
        for q in range(4):
            (nc.scalar if q % 2 else nc.sync).dma_start(
                out=out_2[:, 4 * q : 4 * q + 4, :].bitcast(I32), in_=y_plane[32 * q : 32 * q + 16, :].bitcast(I32)
            )
